import numpy as np, ml_dtypes
CORES = [56,61,80,85]
N = 4
import mx_ref
KO = 1
F = np.float32(0.7)
OWN = [2,2,2,2]
BF = ml_dtypes.bfloat16
def tile(rs):
    return np.stack(rs, axis=2).reshape(128, -1).astype(BF)
def pick(b):
    s = np.zeros((128, 128, 4), np.float32)
    s[np.arange(128), np.arange(128), b] = 1.0
    return mx_ref.quantize(s.reshape(128, 512).astype(BF))
def pk(c, s, i=0):
    return (np.ascontiguousarray(c[:, 512 * i:512 * i + 512]), mx_ref.live(s[:, 128 * i:128 * i + 128]))
def inputs(rng, e, E):
    def f(*shape):
        v = (rng.standard_normal(shape, dtype=np.float32) * np.exp2(rng.integers(-2, 3, shape[:-1] + (1,)))).astype(BF)
        return mx_ref.spread((v.astype(np.float32) * np.exp2(rng.integers(-E, E + 1, shape[:-2] + (1, 1))).astype(np.float32)).astype(BF), rng, e)
    def packed(k):
        c = np.zeros((N, 128, k * 512), np.uint8); s = np.zeros((N, 128, k * 128), np.uint8)
        for r in range(N):
            for i in range(k):
                a, b = mx_ref.quantize(f(128, 512)); c[r][:, 512 * i:512 * i + 512] = a; s[r][:, 128 * i:128 * i + 128] = mx_ref.plane(b, rng)
        return c, s
    d = {}
    d["kc"], d["ks"] = packed(KO)
    d["q"] = f(N, 128, 512)
    return d
def setup_inputs(rng):
    return inputs(rng, 0, 0)
def setup_inputs_blocks(rng):
    return inputs(rng, 4, 0)
def setup_inputs_wide(rng):
    return inputs(rng, 0, 8)
def reference(kc, ks, q):
    S = [pick(t) for t in range(4)]
    anew = lambda p, i: mx_ref.quantize(tile([mx_ref.matmul(S[t], pk(kc[p], ks[p], i)) * F for t in range(4)]))
    y = np.full((N, 128, 512), np.nan, np.float32)
    for o in range(N):
        if OWN[o] != o: continue
        qq = mx_ref.quantize(q[o])
        M = [pk(kc[o], ks[o], i) for i in range(KO)] + [anew(p, i) for p in range(N) if p != o and OWN[p] == o for i in range(KO)]
        y[o][:, :128 * len(M)] = np.concatenate([mx_ref.matmul(qq, m) for m in M], axis=1)
    return {"y": y}

import numpy as np
from concourse.mybir import dt, AluOpType, ActivationFunctionType

C = 128
SCRATCH = {
    "kcod": ("sbuf", [128, C], "float8_e4m3fn_x4"),
    "kpl": ("sbuf", [128, C], "uint8"),
    "ramp": ("sbuf", [128, C], "bfloat16"),
    "e": ("sbuf", [128, 4 * C + 4], "bfloat16"),
    "scod": ("sbuf", [128, 4 * C], "float8_e4m3fn_x4"),
    "spl": ("sbuf", [128, 4 * C], "uint8"),
    "kt": ("sbuf", [128, 4 * C], "bfloat16"),
    "ncod": ("sbuf", [128, C], "float8_e4m3fn_x4"),
    "npl": ("sbuf", [128, C], "uint8"),
    "rcod": ("sbuf", [128, C], "float8_e4m3fn_x4"),
    "rpl": ("sbuf", [128, C], "uint8"),
    "lcod": ("sbuf", [128, 4 * C], "float8_e4m3fn_x4"),
    "lpl": ("sbuf", [128, 4 * C], "uint8"),
    "qt": ("sbuf", [128, 4 * C], "bfloat16"),
    "qcod": ("sbuf", [128, C], "float8_e4m3fn_x4"),
    "qpl": ("sbuf", [128, C], "uint8"),
    "yo": ("sbuf", [128, 4 * C], "float32"),
    "ps": ("psum", [128, 2048], "float32"),
}
SEMAPHORES = ["ld", "lq", "rm", "vz", "vo", "ev", "nq", "sent", "got", "st",
              "s0", "s1", "s2", "s3", "m0", "m1", "m2", "m3", "v0", "v1", "v2", "v3", "a0", "a1", "a2", "a3"]

FACTOR = float(np.float32(0.7))
ENGINES = 8


def engines(topo, src, dst, count):
    full = topo.mask(src, dst)
    bits = [b for b in range(16) if (full >> b) & 1][:count]
    return sum(1 << b for b in bits), len(bits)


def send(g, topo, src, dst, out_ap, in_ap, sem, local, count=ENGINES):
    rid, pid, _ = topo.addr(dst)
    m, n = engines(topo, src, dst, count)
    g.remote_dma(out_ap=out_ap, in_ap=in_ap, remote_sem=sem, local_sem=local, pid=pid, routing_id=rid, dma_engine_mask=m)
    return n


def raw(ap):
    return ap.bitcast(dt.uint8)


def plan(T, topo):
    own = T.tables["OWN"]
    taken = set(T.cores)
    ways = {}
    for p in range(len(own)):
        o = own[p]
        if o == p:
            continue
        place = 1 + [r for r in range(len(own)) if r != o and own[r] == o].index(p)
        pc, oc = T.cores[p], T.cores[o]
        if topo.may_write(pc, oc):
            ways[p] = (o, place, None)
            continue
        cand = [c for c in range(96) if c not in taken and topo.chip(c) == topo.chip(pc) and topo.may_write(c, oc)]
        cand.sort(key=lambda c: (topo.die(c) != topo.die(pc), c))
        taken.update(cand[:2])
        ways[p] = (o, place, (cand[0], cand[1]))
    return ways


def producer(g, core, T, topo, way):
    o, place, relays = way
    s = T.sem
    oc = T.cores[o]
    g.sync.dma_start(raw(T.kcod[:]), T.kc[:]).then_inc(s.ld, 16)
    g.scalar.dma_start(T.kpl[:], T.ks[:]).then_inc(s.ld, 16)
    g.iota(T.ramp[:], [[-1, C]], 0, 1, allow_small_or_imprecise_dtypes=True).then_inc(s.rm, 1)
    g.vector.memset(T.e[:], 0.0).then_inc(s.vz, 1)
    g.vector.wait_ge(s.vz, 1)
    g.vector.wait_ge(s.rm, 1)
    g.vector.tensor_scalar(T.e[:, 3:4 * C + 3:4], T.ramp[:], 0.0, None, AluOpType.is_equal).then_inc(s.vo, 1)
    g.vector.wait_ge(s.vo, 1)
    for b in range(4):
        g.vector.quantize_mx(T.scod[:, C * b:C * b + C], T.spl[:, C * b:C * b + C], T.e[:, 3 - b:3 - b + 4 * C]).then_inc(s["s%d" % b], 1)
    g.tensor.wait_ge(s.ld, 32)
    for b in range(4):
        g.tensor.wait_ge(s["s%d" % b], 1)
        g.tensor.matmul_mx(T.ps[:, 512 * b:512 * b + C], T.scod[:, C * b:C * b + C], T.spl[:, C * b:C * b + C],
                           T.kcod[:], T.kpl[:], True, True).then_inc(s["m%d" % b], 1)
    for b in range(4):
        out, in_ = T.kt[:, b:4 * C:4], T.ps[:, 512 * b:512 * b + C]
        if b % 2 == 0:
            g.scalar.wait_ge(s["m%d" % b], 1)
            g.scalar.activation(out, in_, ActivationFunctionType.Copy, scale=FACTOR).then_inc(s.ev, 1)
        else:
            g.vector.wait_ge(s["m%d" % b], 1)
            g.vector.tensor_scalar(out, in_, FACTOR, None, AluOpType.mult).then_inc(s.ev, 1)
    g.vector.wait_ge(s.ev, 4)
    g.vector.quantize_mx(T.ncod[:], T.npl[:], T.kt[:]).then_inc(s.nq, 1)
    g.wait_ge(s.nq, 1)
    if relays is None:
        lo, hi = C * place, C * place + C
        arr = s["a%d" % place]
        n = send(g, topo, core, oc, raw(T.lcod[:, lo:hi]), raw(T.ncod[:]), arr, s.sent)
        n += send(g, topo, core, oc, T.lpl[:, lo:hi], T.npl[:], arr, s.sent)
    else:
        n = send(g, topo, core, relays[0], raw(T.rcod[:]), raw(T.ncod[:]), s.got, s.sent)
        n += send(g, topo, core, relays[1], T.rpl[:], T.npl[:], s.got, s.sent)
    g.wait_ge(s.sent, n)


def relay(g, core, T, topo, p, way, which):
    o, place, relays = way
    s = T.sem
    lo, hi = C * place, C * place + C
    g.wait_ge(s.got, engines(topo, T.cores[p], core, ENGINES)[1])
    if which == 0:
        out_ap, in_ap = raw(T.lcod[:, lo:hi]), raw(T.rcod[:])
    else:
        out_ap, in_ap = T.lpl[:, lo:hi], T.rpl[:]
    n = send(g, topo, core, T.cores[o], out_ap, in_ap, s["a%d" % place], s.sent)
    g.wait_ge(s.sent, n)


def consumer(g, core, rank, T, topo, ways):
    s = T.sem
    g.sync.dma_start(T.qt[:], T.q[:]).then_inc(s.lq, 16)
    g.scalar.dma_start(raw(T.kcod[:]), T.kc[:]).then_inc(s.ld, 16)
    g.scalar.dma_start(T.kpl[:], T.ks[:]).then_inc(s.ld, 16)
    g.vector.wait_ge(s.lq, 16)
    g.vector.quantize_mx(T.qcod[:], T.qpl[:], T.qt[:]).then_inc(s.nq, 1)
    mine = sorted([(w[2] is not None, w[1], p) for p, w in ways.items() if w[0] == rank])
    order = [0] + [place for _, place, _ in mine]
    count = {}
    for _, place, p in mine:
        w = ways[p]
        count[place] = sum(engines(topo, src, core, ENGINES)[1] for src in (w[2] or (T.cores[p], T.cores[p])))
    g.tensor.wait_ge(s.nq, 1)
    for i in order:
        if i == 0:
            g.tensor.wait_ge(s.ld, 32)
            mov, pl = T.kcod[:], T.kpl[:]
        else:
            g.tensor.wait_ge(s["a%d" % i], count[i])
            mov, pl = T.lcod[:, C * i:C * i + C], T.lpl[:, C * i:C * i + C]
        g.tensor.matmul_mx(T.ps[:, 512 * i:512 * i + C], T.qcod[:], T.qpl[:], mov, pl, True, True).then_inc(s["m%d" % i], 1)
    for i in order:
        out, in_ = T.yo[:, C * i:C * i + C], T.ps[:, 512 * i:512 * i + C]
        if i == order[-1]:
            g.scalar.wait_ge(s["m%d" % i], 1)
            g.scalar.activation(out, in_, ActivationFunctionType.Copy).then_inc(s["v%d" % i], 1)
            q = g.scalar
        else:
            g.vector.wait_ge(s["m%d" % i], 1)
            g.vector.tensor_copy(out, in_).then_inc(s["v%d" % i], 1)
            q = g.sync
        q.wait_ge(s["v%d" % i], 1)
        q.dma_start(T.y[:, C * i:C * i + C], out).then_inc(s.st, 16)
    g.sync.wait_ge(s.st, 16 * len(order))


def rank_program(g, core, T, topo):
    ways = plan(T, topo)
    rank = T.rank_of(core)
    if rank is None:
        for p, w in ways.items():
            if w[2] is not None and core in w[2]:
                relay(g, core, T, topo, p, w, w[2].index(core))
    elif rank in ways:
        producer(g, core, T, topo, ways[rank])
    else:
        consumer(g, core, rank, T, topo, ways)
